import numpy as np
import ml_dtypes


def mxq(x, axis, fmt="e4m3"):
    dtype, down = {"e4m3": (ml_dtypes.float8_e4m3fn, 7), "e5m2": (ml_dtypes.float8_e5m2, 14)}[fmt]
    v = np.moveaxis(np.asarray(x, np.float32).astype(ml_dtypes.bfloat16).astype(np.float64), axis, -1)
    blocks = v.reshape(v.shape[:-1] + (-1, 32))
    amax = np.abs(blocks).max(-1, keepdims=True)
    byte = np.maximum(np.where(amax > 0, np.frexp(amax)[1] - 1 + 127, 0) - down, 1)
    scale = np.exp2(byte - 127.0)
    codes = (blocks / scale).astype(np.float32).astype(dtype).astype(np.float64)
    return np.moveaxis((codes * scale).reshape(v.shape), -1, axis)


WIDE = False


def mx_kscale(k):
    if not WIDE:
        return np.ones(k)
    levels = np.array([10, -10, 5, -5, 0])
    if k % 512:
        return np.exp2(np.random.permutation(np.resize(levels, k // 32))).repeat(32)
    a = np.empty((k // 512, 16))
    for p in range(k // 512):
        a[p, :8] = np.random.permutation(np.resize(levels, 8))
        for g in range(8):
            far = levels[np.abs(levels - a[p, g]) >= 10]
            a[p, g + 8] = far[np.random.randint(len(far))]
    return np.exp2(a.ravel()).repeat(32)


BF16 = ml_dtypes.bfloat16


def bf(x):
    return np.asarray(x, np.float32).astype(BF16)


def f64(x):
    return np.asarray(x).astype(np.float64)

def planes(Y):
    n, m = Y.shape
    b = f64(bf(Y)).reshape(n // 32, 32, m)
    amax = np.abs(b).max(1)
    byte = np.clip(np.where(amax > 0, np.frexp(amax)[1] - 1 + 127 - 7, 1), 1, 254)
    codes = (b * np.exp2(127.0 - byte)[:, None, :]).reshape(n, m).astype(np.float32).astype(ml_dtypes.float8_e4m3fn).view(np.uint8)
    words = codes.reshape(n // 512, 128, 4, m).transpose(0, 1, 3, 2)
    return np.ascontiguousarray(words), np.ascontiguousarray(byte.astype(np.uint8).reshape(n // 512, 16, m))


B, S, D = 1, 1024, 512


def log_normalise(l, axis):
    m = np.max(l, axis=axis, keepdims=True)
    lse = m + np.log(np.sum(np.exp(l - m), axis=axis, keepdims=True))
    return l - lse


def setup_inputs():
    s, t = mx_kscale(D), mx_kscale(S)
    q = np.random.standard_normal((B, S, D)) * s
    k = np.random.standard_normal((B, S, D)) / s
    v = np.random.standard_normal((B, S, D)) / t[:, None]
    pos = np.random.standard_normal((S, S)) + np.random.standard_normal((S, 1)) + 0.7 * np.random.standard_normal((1, S))
    g = (1.0 + 0.1 * np.random.standard_normal(S)) * t
    return {"q": bf(q), "k": bf(k), "v": bf(v), "pos": bf(pos), "g": bf(g)}


def core(q, k, v, pos, g):
    qq = mxq(f64(q), 2, "e4m3")
    kq = mxq(f64(k), 2, "e4m3")
    l = (1.5 / np.sqrt(D)) * (qq @ kq.transpose(0, 2, 1)) + f64(pos)[None, :, :]
    l1 = log_normalise(l, -1)
    l2 = log_normalise(l1, 1)
    l3 = log_normalise(l2, -1)
    p = np.exp(l3)
    c = ((S * p - 1.0) / np.sqrt(S)) * f64(g)[None, None, :]
    return mxq(c, 2, "e4m3") @ mxq(f64(v), 1, "e4m3")


def reference(q, k, v, pos, g):
    R_out = core(q, k, v, pos, g)
    words, scales = planes(np.moveaxis(R_out, 1, 0).reshape(1024, -1))
    return R_out, words, scales

@@ -1,0 +1,343 @@
+from contextlib import ExitStack
+
+import concourse.mybir as mybir
+from concourse.masks import make_identity
+
+F32 = mybir.dt.float32
+BF16 = mybir.dt.bfloat16
+U32 = mybir.dt.uint32
+I32 = mybir.dt.int32
+U8 = mybir.dt.uint8
+FP8X4 = mybir.dt.float8_e4m3fn_x4
+ALU = mybir.AluOpType
+ACT = mybir.ActivationFunctionType
+
+S = 1024
+D = 512
+P = 128
+NT = 8
+ALPHA = 1.5 / (D ** 0.5)
+
+FLOPS = 2 * 2 * S * S * D
+
+
+def tile_sinkhorndoublystochastictokenmixer_x1_kernel(tc, q, k, v, pos, g, out_0, out_1, out_2):
+    nc = tc.nc
+    with ExitStack() as ctx:
+        one = ctx.enter_context(tc.tile_pool(name="one", bufs=1))
+        eight = ctx.enter_context(tc.tile_pool(name="eight", bufs=8))
+        three = ctx.enter_context(tc.tile_pool(name="three", bufs=3))
+        psl = ctx.enter_context(tc.psum_pool(name="psl", bufs=4))
+        pst = ctx.enter_context(tc.psum_pool(name="pst", bufs=2))
+        psa = ctx.enter_context(tc.psum_pool(name="psa", bufs=2))
+        ctx.enter_context(tc.manual_schedule())
+
+        k_sb = [one.tile([P, 4, D], BF16, name="k_sb%d" % i, align_bytes=64) for i in range(2)]
+        q_sb = [one.tile([P, 4, D], BF16, name="q_sb%d" % i, align_bytes=64) for i in range(2)]
+        v_sb = [one.tile([P, 4, D], BF16, name="v_sb%d" % i, align_bytes=64) for i in range(2)]
+        pos_sb = [eight.tile([P, S], BF16, name="pos_sb", align_bytes=64) for i in range(NT)]
+        g_sb = one.tile([P, 2, 4], BF16, name="g_sb")
+        kv = k[0, :, :].rearrange("(g p t) d -> g p t d", g=2, t=4)
+        qv = q[0, :, :].rearrange("(g p t) d -> g p t d", g=2, t=4)
+        vv = v[0, :, :].rearrange("(g p t) d -> g p t d", g=2, t=4)
+        posv = pos.rearrange("(g p t) j -> g p t j", g=2, t=4)
+
+        def load(dst, src, gi, lo, hi):
+            nc.sync.dma_start(out=dst[gi][:, lo:hi, :], in_=src[gi, :, lo:hi, :])
+
+        def load_pos(t):
+            nc.sync.dma_start(out=pos_sb[t][:], in_=posv[t // 4, :, t % 4, :])
+
+        load(k_sb, kv, 0, 0, 2)
+        load(k_sb, kv, 0, 2, 4)
+        load(q_sb, qv, 0, 0, 2)
+        load(k_sb, kv, 1, 0, 2)
+        load(k_sb, kv, 1, 2, 4)
+        load_pos(0)
+        load_pos(1)
+        load(q_sb, qv, 0, 2, 4)
+        load_pos(2)
+        load_pos(3)
+        load(q_sb, qv, 1, 0, 4)
+        load_pos(4)
+        load_pos(5)
+        load_pos(6)
+        load_pos(7)
+        load(v_sb, vv, 0, 0, 4)
+        load(v_sb, vv, 1, 0, 4)
+        nc.sync.dma_start(out=g_sb[:], in_=g.rearrange("(g p t) -> p g t", g=2, t=4))
+
+        ident = one.tile([P, P], F32, name="ident")
+        make_identity(nc, ident[:])
+
+        k_gr = [one.tile([P, 512, 4], BF16, name="k_gr%d" % i, align_bytes=64) for i in range(2)]
+        k_c = [one.tile([P, 512], U32, name="k_c%d" % i, align_bytes=64) for i in range(2)]
+        k_s = [one.tile([P, 512], U8, name="k_s%d" % i, align_bytes=64) for i in range(2)]
+        q_gr = [one.tile([P, 256, 4], BF16, name="q_gr%d" % i, align_bytes=64) for i in range(4)]
+        q_c = [one.tile([P, 256], U32, name="q_c%d" % i, align_bytes=64) for i in range(4)]
+        q_s = [one.tile([P, 256], U8, name="q_s%d" % i, align_bytes=64) for i in range(4)]
+        v_gr = [one.tile([P, D, 4], BF16, name="v_gr%d" % i, align_bytes=64) for i in range(2)]
+        v_c = [one.tile([P, D], U32, name="v_c%d" % i, align_bytes=64) for i in range(2)]
+        v_s = [one.tile([P, D], U8, name="v_s%d" % i, align_bytes=64) for i in range(2)]
+
+        def turn_pair(src, t0):
+            bank = pst.tile([P, 2, 256], F32, name="tp")
+            for tt in range(2):
+                words = src[:, t0 + tt, :].bitcast(F32)
+                for u in range(2):
+                    nc.tensor.transpose(bank[:, u, tt * P:(tt + 1) * P], words[:, u:256:2], ident[:])
+            return bank
+
+        def move_words(copy, bank, dst):
+            copy(out=dst.rearrange("p r j -> p (r j)").bitcast(F32).rearrange("p (r u) -> p r u", u=2),
+                 in_=bank[:].rearrange("p u r -> p r u"))
+
+        def quant(gr, codes, scales):
+            nc.vector.quantize_mx(out=codes[:].bitcast(FP8X4), scales=scales[:],
+                                  in_=gr[:].rearrange("p r j -> p (r j)"))
+
+        def q_turn(h):
+            bank = turn_pair(q_sb[h // 2], (h % 2) * 2)
+            move_words(nc.scalar.copy, bank, q_gr[h][:])
+
+        def k_turn(gi):
+            b0 = turn_pair(k_sb[gi], 0)
+            move_words(nc.scalar.copy, b0, k_gr[gi][:, 0:256, :])
+            b1 = turn_pair(k_sb[gi], 2)
+            move_words(nc.vector.tensor_copy if gi == 0 else nc.scalar.copy, b1, k_gr[gi][:, 256:512, :])
+
+        lp = {}
+
+        def scores(t, half=(0, 1)):
+            h = t // 2
+            cols = slice((t % 2) * P, (t % 2 + 1) * P)
+            for gj in half:
+                bank = psl.tile([P, 512], F32, name="lp")
+                nc.tensor.matmul_mx(out=bank[:], lhsT=q_c[h][:, cols].bitcast(FP8X4), lhsT_scale=q_s[h][:, cols],
+                                    rhs=k_c[gj][:].bitcast(FP8X4), rhs_scale=k_s[gj][:], start=True, stop=True)
+                lp[t, gj] = bank
+
+        neg_l = {}
+        neg_m = {}
+        e = {}
+        row = {}
+        rinv = {}
+
+        def add_pos(t, halves=(0, 1)):
+            if t not in neg_l:
+                nl = three.tile([P, S], F32, name="nl")
+                neg_l[t] = nl
+            nl = neg_l[t]
+            for gj in halves:
+                half = slice(gj * 512, (gj + 1) * 512)
+                nc.vector.scalar_tensor_tensor(
+                    out=nl[:, half].rearrange("p (t a) -> p t a", t=4),
+                    in0=lp[t, gj][:].rearrange("p (t a) -> p t a", t=4),
+                    scalar=-ALPHA,
+                    in1=pos_sb[t][:, half].rearrange("p (a t) -> p t a", t=4),
+                    op0=ALU.mult, op1=ALU.subtract)
+
+        def row_max(t):
+            junk = three.tile([P, S], F32, name="junk")
+            nm = eight.tile([P, 1], F32, name="nm")
+            nc.vector.tensor_scalar(out=junk[:], in0=neg_l[t][:], scalar1=1.0, scalar2=None,
+                                    op0=ALU.mult, op1=ALU.min, accum_out=nm[:])
+            neg_m[t] = nm
+
+        def expo(t):
+            et = eight.tile([P, S], F32, name="et")
+            rt = eight.tile([P, 1], F32, name="rt")
+            nc.scalar.activation(out=et[:], in_=neg_l[t][:], func=ACT.Exp, bias=neg_m[t][:], scale=-1.0,
+                                 accum_out=rt[:])
+            e[t] = et
+            row[t] = rt
+
+        def row_norm(t):
+            ri = eight.tile([P, 1], F32, name="ri")
+            nc.vector.reciprocal(out=ri[:], in_=row[t][:])
+            rinv[t] = ri
+
+        acc = [psa.tile([P, 4], F32, name="acc") for i in range(2)]
+
+        def col_add(t):
+            for gj in range(2):
+                for tj in range(4):
+                    c0 = (gj * 4 + tj) * P
+                    nc.tensor.matmul(out=acc[gj][:, tj:tj + 1], lhsT=e[t][:, c0:c0 + P], rhs=rinv[t][:],
+                                     start=(t == 0 and tj == 0), stop=(t == NT - 1 and tj == 3))
+
+        k_turn(0)
+        q_turn(0)
+        quant(k_gr[0], k_c[0], k_s[0])
+        quant(q_gr[0], q_c[0], q_s[0])
+        k_turn(1)
+        scores(0, (0,))
+        scores(1, (0,))
+        q_turn(1)
+        add_pos(0, (0,))
+        add_pos(1, (0,))
+        quant(k_gr[1], k_c[1], k_s[1])
+        scores(0, (1,))
+        scores(1, (1,))
+
+        def v_move(gi, part, copy):
+            cols = slice(part * 256, (part + 1) * 256)
+            copy(out=v_gr[gi][:, cols, :], in_=v_sb[gi][:, :, cols].rearrange("p t d -> p d t"))
+
+        for t in range(NT):
+            more = t % 2 == 0 and t < 6
+            add_pos(t, (1,) if t < 2 else (0, 1))
+            row_max(t)
+            expo(t)
+            if t == 1 or t == 3:
+                q_turn(t // 2 + 2)
+            if more:
+                h = t // 2 + 1
+                quant(q_gr[h], q_c[h], q_s[h])
+            if t + 2 < NT:
+                scores(t + 2)
+            if t > 0:
+                row_norm(t - 1)
+                col_add(t - 1)
+            if t == 3 or t == 5:
+                v_move(0, (t - 3) // 2, nc.scalar.copy)
+        quant(v_gr[0], v_c[0], v_s[0])
+        v_move(1, 0, nc.vector.tensor_copy)
+        row_norm(NT - 1)
+        col_add(NT - 1)
+        v_move(1, 1, nc.vector.tensor_copy)
+        quant(v_gr[1], v_c[1], v_s[1])
+
+        u = one.tile([P, 8], F32, name="u")
+        ub = one.tile([P, S], F32, name="ub")
+        for gj in range(2):
+            cols = slice(gj * 4, (gj + 1) * 4)
+            nc.vector.reciprocal(out=u[:, cols], in_=acc[gj][:])
+            bank = pst.tile([P, 512], F32, name="tp")
+            for tj in range(4):
+                b = gj * 4 + tj
+                nc.tensor.transpose(bank[:, tj * P:(tj + 1) * P], u[:, b:b + 1].to_broadcast([P, P]), ident[:])
+            (nc.vector.tensor_copy if gj else nc.scalar.copy)(out=ub[:, gj * 512:(gj + 1) * 512], in_=bank[:])
+        g32 = one.tile([P, 8], F32, name="g32")
+        nc.vector.tensor_scalar(out=g32[:], in0=g_sb[:].rearrange("p g t -> p (g t)"), scalar1=S / (S ** 0.5),
+                                scalar2=None, op0=ALU.mult)
+
+        w = {}
+        sinv = {}
+        x = {}
+        xt = {}
+        c_gr = {}
+        c_c = {}
+        c_s = {}
+        o32 = {}
+        o_ps = {}
+
+        def col_norm(t):
+            wt = three.tile([P, S], F32, name="wt")
+            st = eight.tile([P, 1], F32, name="st")
+            nc.vector.scalar_tensor_tensor(out=wt[:], in0=e[t][:], scalar=1.0, in1=ub[:], op0=ALU.mult, op1=ALU.mult,
+                                           accum_out=st[:])
+            si = eight.tile([P, 1], F32, name="si")
+            nc.vector.reciprocal(out=si[:], in_=st[:])
+            w[t] = wt
+            sinv[t] = si
+
+        def row_scale(t):
+            xx = three.tile([P, S], F32, name="xx")
+            nc.scalar.activation(out=xx[:], in_=w[t][:], func=ACT.Copy, bias=-1.0 / S, scale=sinv[t][:])
+            x[t] = xx
+
+        def turn_mix(t):
+            for gj in range(2):
+                bank = psl.tile([P, 4, P], F32, name="lp")
+                for tj in range(4):
+                    c0 = (gj * 4 + tj) * P
+                    nc.tensor.transpose(bank[:, tj, :], x[t][:, c0:c0 + P], ident[:])
+                xt[t, gj] = bank
+
+        def gain(t):
+            cg = three.tile([P, 2, P, 4], BF16, name="cg", align_bytes=64)
+            for gj in range(2):
+                nc.vector.tensor_tensor(
+                    out=cg[:, gj, :, :],
+                    in0=xt[t, gj][:].rearrange("p t i -> p i t"),
+                    in1=g32[:, gj * 4:(gj + 1) * 4].unsqueeze(1).to_broadcast([P, P, 4]),
+                    op=ALU.mult)
+            c_gr[t] = cg
+
+        def quant_c(t):
+            cc = three.tile([P, 256], U32, name="cc", align_bytes=64)
+            cs = three.tile([P, 256], U8, name="cs", align_bytes=64)
+            nc.vector.quantize_mx(out=cc[:].bitcast(FP8X4), scales=cs[:],
+                                  in_=c_gr[t][:].rearrange("p g i t -> p (g i t)"))
+            c_c[t] = cc
+            c_s[t] = cs
+
+        def mix_part(t, bank, lo, hi):
+            for gj in range(2):
+                cols = slice(gj * P, (gj + 1) * P)
+                nc.tensor.matmul_mx(out=bank[:, 0:hi - lo], lhsT=c_c[t][:, cols].bitcast(FP8X4),
+                                    lhsT_scale=c_s[t][:, cols],
+                                    rhs=v_c[gj][:, lo:hi].bitcast(FP8X4), rhs_scale=v_s[gj][:, lo:hi],
+                                    start=(gj == 0), stop=(gj == 1))
+
+        def mix(t):
+            bank = psa.tile([P, 512], F32, name="acc")
+            mix_part(t, bank, 0, D)
+            o_ps[t] = bank
+
+        outv = out_0[0, :, :].rearrange("(g p t) d -> g p t d", g=2, t=4)
+        o_sb = [one.tile([P, 4, D], F32, name="o_sb%d" % i) for i in range(2)]
+        o_gr = [one.tile([P, D, 4], BF16, name="o_gr%d" % i, align_bytes=64) for i in range(2)]
+        o_c = [one.tile([P, D], U32, name="o_c%d" % i, align_bytes=64) for i in range(2)]
+        o_s = [one.tile([P, D], U8, name="o_s%d" % i, align_bytes=64) for i in range(2)]
+
+        def leave(t):
+            nc.scalar.copy(out=o_sb[t // 4][:, t % 4, :], in_=o_ps[t][:])
+            nc.sync.dma_start(out=outv[t // 4, :, t % 4, :], in_=o_sb[t // 4][:, t % 4, :])
+
+        def group_move(gi, lo, hi, copy):
+            cols = slice(lo, hi)
+            copy(out=o_gr[gi][:, cols, :], in_=o_sb[gi][:, :, cols].rearrange("p t d -> p d t"))
+
+        def group_out(gi):
+            for part in range(2):
+                cols = slice(part * 256, (part + 1) * 256)
+                nc.vector.quantize_mx(out=o_c[gi][:, cols].bitcast(FP8X4), scales=o_s[gi][:, cols],
+                                      in_=o_gr[gi][:, cols, :].rearrange("p m t -> p (m t)"))
+            nc.sync.dma_start(out=out_1[gi, :, :, :].rearrange("p m t -> p (m t)").bitcast(I32),
+                              in_=o_c[gi][:].bitcast(I32))
+            for qd in range(4):
+                nc.sync.dma_start(out=out_2[gi, 4 * qd:4 * qd + 4, :].bitcast(I32),
+                                  in_=o_s[gi][32 * qd:32 * qd + 4, :].bitcast(I32))
+
+        for t in range(3):
+            col_norm(t)
+            row_scale(t)
+            if t < 2:
+                turn_mix(t)
+        for t in range(NT):
+            gain(t)
+            if t + 2 < NT:
+                turn_mix(t + 2)
+            if t + 3 < NT:
+                col_norm(t + 3)
+                row_scale(t + 3)
+            quant_c(t)
+            if t < NT - 1:
+                mix(t)
+                leave(t)
+            if t == 4 or t == 5:
+                group_move(0, (t - 4) * 256, (t - 3) * 256, nc.scalar.copy)
+        last = NT - 1
+        low = psa.tile([P, 512], F32, name="acc")
+        high = pst.tile([P, 512], F32, name="tp")
+        mix_part(last, low, 0, 256)
+        mix_part(last, high, 256, 512)
+        group_out(0)
+        nc.vector.tensor_copy(out=o_sb[1][:, 3, 0:256], in_=low[:, 0:256])
+        nc.scalar.copy(out=o_sb[1][:, 3, 256:512], in_=high[:, 0:256])
+        nc.sync.dma_start(out=outv[1, :, 3, :], in_=o_sb[1][:, 3, :])
+        group_move(1, 0, 320, nc.vector.tensor_copy)
+        group_move(1, 320, 512, nc.scalar.copy)
+        group_out(1)

@@ -18,6 +18,9 @@ P = 128
 NT = 8
 ALPHA = 1.5 / (D ** 0.5)
 
+SHIFT = 40.0
+GROW = float(2 ** 56)
+
 FLOPS = 2 * 2 * S * S * D
 
 
@@ -48,9 +51,9 @@ def tile_sinkhorndoublystochastictokenmixer_x1_kernel(tc, q, k, v, pos, g, out_0
         def load_pos(t):
             nc.sync.dma_start(out=pos_sb[t][:], in_=posv[t // 4, :, t % 4, :])
 
+        load(q_sb, qv, 0, 0, 2)
         load(k_sb, kv, 0, 0, 2)
         load(k_sb, kv, 0, 2, 4)
-        load(q_sb, qv, 0, 0, 2)
         load(k_sb, kv, 1, 0, 2)
         load(k_sb, kv, 1, 2, 4)
         load_pos(0)
@@ -80,8 +83,8 @@ def tile_sinkhorndoublystochastictokenmixer_x1_kernel(tc, q, k, v, pos, g, out_0
         v_c = [one.tile([P, D], U32, name="v_c%d" % i, align_bytes=64) for i in range(2)]
         v_s = [one.tile([P, D], U8, name="v_s%d" % i, align_bytes=64) for i in range(2)]
 
-        def turn_pair(src, t0):
-            bank = pst.tile([P, 2, 256], F32, name="tp")
+        def turn_pair(src, t0, pool=pst, name="tp"):
+            bank = pool.tile([P, 2, 256], F32, name=name)
             for tt in range(2):
                 words = src[:, t0 + tt, :].bitcast(F32)
                 for u in range(2):
@@ -96,15 +99,18 @@ def tile_sinkhorndoublystochastictokenmixer_x1_kernel(tc, q, k, v, pos, g, out_0
             nc.vector.quantize_mx(out=codes[:].bitcast(FP8X4), scales=scales[:],
                                   in_=gr[:].rearrange("p r j -> p (r j)"))
 
-        def q_turn(h):
-            bank = turn_pair(q_sb[h // 2], (h % 2) * 2)
-            move_words(nc.scalar.copy, bank, q_gr[h][:])
+        def q_turn(h, copy=nc.scalar.copy, **where):
+            bank = turn_pair(q_sb[h // 2], (h % 2) * 2, **where)
+            move_words(copy, bank, q_gr[h][:])
 
-        def k_turn(gi):
-            b0 = turn_pair(k_sb[gi], 0)
-            move_words(nc.scalar.copy, b0, k_gr[gi][:, 0:256, :])
-            b1 = turn_pair(k_sb[gi], 2)
-            move_words(nc.vector.tensor_copy if gi == 0 else nc.scalar.copy, b1, k_gr[gi][:, 256:512, :])
+        def k_turn(gi, half, copy, **where):
+            bank = turn_pair(k_sb[gi], 2 * half, **where)
+            move_words(copy, bank, k_gr[gi][:, half * 256:(half + 1) * 256, :])
+
+        def k_quant(gi, half):
+            cols = slice(half * 256, (half + 1) * 256)
+            nc.vector.quantize_mx(out=k_c[gi][:, cols].bitcast(FP8X4), scales=k_s[gi][:, cols],
+                                  in_=k_gr[gi][:, cols, :].rearrange("p r j -> p (r j)"))
 
         lp = {}
 
@@ -140,8 +146,8 @@ def tile_sinkhorndoublystochastictokenmixer_x1_kernel(tc, q, k, v, pos, g, out_0
         def row_max(t):
             junk = three.tile([P, S], F32, name="junk")
             nm = eight.tile([P, 1], F32, name="nm")
-            nc.vector.tensor_scalar(out=junk[:], in0=neg_l[t][:], scalar1=1.0, scalar2=None,
-                                    op0=ALU.mult, op1=ALU.min, accum_out=nm[:])
+            nc.vector.tensor_scalar(out=junk[:], in0=neg_l[t][:], scalar1=SHIFT, scalar2=None,
+                                    op0=ALU.add, op1=ALU.min, accum_out=nm[:])
             neg_m[t] = nm
 
         def expo(t):
@@ -152,31 +158,44 @@ def tile_sinkhorndoublystochastictokenmixer_x1_kernel(tc, q, k, v, pos, g, out_0
             e[t] = et
             row[t] = rt
 
-        def row_norm(t):
+        def row_recip(t):
             ri = eight.tile([P, 1], F32, name="ri")
             nc.vector.reciprocal(out=ri[:], in_=row[t][:])
             rinv[t] = ri
 
-        acc = [psa.tile([P, 4], F32, name="acc") for i in range(2)]
+        def row_norm(t):
+            ri = rinv[t]
+            eng = nc.vector if t >= NT - 2 else nc.gpsimd
+            pieces = 2 if t == NT - 1 else 1
+            for n in range(pieces):
+                part = slice(n * S // pieces, (n + 1) * S // pieces)
+                eng.tensor_scalar(out=e[t][:, part], in0=e[t][:, part], scalar1=GROW, scalar2=ri[:],
+                                  op0=ALU.mult, op1=ALU.mult)
+
+        acc = [psa.tile([P, 4, P], F32, name="acc") for i in range(2)]
 
         def col_add(t):
             for gj in range(2):
                 for tj in range(4):
                     c0 = (gj * 4 + tj) * P
-                    nc.tensor.matmul(out=acc[gj][:, tj:tj + 1], lhsT=e[t][:, c0:c0 + P], rhs=rinv[t][:],
-                                     start=(t == 0 and tj == 0), stop=(t == NT - 1 and tj == 3))
+                    nc.tensor.matmul(out=acc[gj][:, tj, :], lhsT=e[t][:, c0:c0 + P], rhs=ident[:],
+                                     start=(t == 0 and tj == 0), stop=(t == NT - 1 and tj == 3), is_transpose=True)
 
-        k_turn(0)
-        q_turn(0)
-        quant(k_gr[0], k_c[0], k_s[0])
+        q_turn(0, nc.vector.tensor_copy)
+        k_turn(0, 0, nc.scalar.copy)
         quant(q_gr[0], q_c[0], q_s[0])
-        k_turn(1)
+        k_turn(0, 1, nc.vector.tensor_copy, pool=psl, name="lp")
+        k_quant(0, 0)
+        k_quant(0, 1)
+        k_turn(1, 0, nc.scalar.copy, pool=psl, name="lp")
+        k_turn(1, 1, nc.scalar.copy)
         scores(0, (0,))
         scores(1, (0,))
         q_turn(1)
         add_pos(0, (0,))
+        k_quant(1, 0)
+        k_quant(1, 1)
         add_pos(1, (0,))
-        quant(k_gr[1], k_c[1], k_s[1])
         scores(0, (1,))
         scores(1, (1,))
 
@@ -185,45 +204,53 @@ def tile_sinkhorndoublystochastictokenmixer_x1_kernel(tc, q, k, v, pos, g, out_0
             copy(out=v_gr[gi][:, cols, :], in_=v_sb[gi][:, :, cols].rearrange("p t d -> p d t"))
 
         for t in range(NT):
-            more = t % 2 == 0 and t < 6
-            add_pos(t, (1,) if t < 2 else (0, 1))
-            row_max(t)
-            expo(t)
             if t == 1 or t == 3:
                 q_turn(t // 2 + 2)
-            if more:
+            add_pos(t, (1,))
+            if t > 0 and t + 1 < NT:
+                add_pos(t + 1, (0,))
+            row_max(t)
+            expo(t)
+            if t % 2 == 0 and t < 6:
                 h = t // 2 + 1
                 quant(q_gr[h], q_c[h], q_s[h])
+            if t > 0:
+                row_recip(t - 1)
+                row_norm(t - 1)
             if t + 2 < NT:
                 scores(t + 2)
             if t > 0:
-                row_norm(t - 1)
                 col_add(t - 1)
             if t == 3 or t == 5:
                 v_move(0, (t - 3) // 2, nc.scalar.copy)
         quant(v_gr[0], v_c[0], v_s[0])
-        v_move(1, 0, nc.vector.tensor_copy)
+        g32 = one.tile([P, 8], F32, name="g32")
+        nc.vector.tensor_scalar(out=g32[:], in0=g_sb[:].rearrange("p g t -> p (g t)"), scalar1=S / (S ** 0.5),
+                                scalar2=None, op0=ALU.mult)
+        row_recip(NT - 1)
         row_norm(NT - 1)
         col_add(NT - 1)
-        v_move(1, 1, nc.vector.tensor_copy)
-        quant(v_gr[1], v_c[1], v_s[1])
+        v_move(1, 0, nc.scalar.copy)
+        v_move(1, 1, nc.scalar.copy)
 
         u = one.tile([P, 8], F32, name="u")
+        csum = one.tile([P, 8], F32, name="csum")
         ub = one.tile([P, S], F32, name="ub")
         for gj in range(2):
             cols = slice(gj * 4, (gj + 1) * 4)
-            nc.vector.reciprocal(out=u[:, cols], in_=acc[gj][:])
+            nc.vector.tensor_reduce(out=csum[:, cols], in_=acc[gj][:], axis=mybir.AxisListType.X, op=ALU.add)
+            nc.vector.reciprocal(out=u[:, cols], in_=csum[:, cols])
+            if gj == 1:
+                quant(v_gr[1], v_c[1], v_s[1])
             bank = pst.tile([P, 512], F32, name="tp")
             for tj in range(4):
                 b = gj * 4 + tj
                 nc.tensor.transpose(bank[:, tj * P:(tj + 1) * P], u[:, b:b + 1].to_broadcast([P, P]), ident[:])
             (nc.vector.tensor_copy if gj else nc.scalar.copy)(out=ub[:, gj * 512:(gj + 1) * 512], in_=bank[:])
-        g32 = one.tile([P, 8], F32, name="g32")
-        nc.vector.tensor_scalar(out=g32[:], in0=g_sb[:].rearrange("p g t -> p (g t)"), scalar1=S / (S ** 0.5),
-                                scalar2=None, op0=ALU.mult)
 
         w = {}
         sinv = {}
+        rsum = {}
         x = {}
         xt = {}
         c_gr = {}
@@ -237,9 +264,12 @@ def tile_sinkhorndoublystochastictokenmixer_x1_kernel(tc, q, k, v, pos, g, out_0
             st = eight.tile([P, 1], F32, name="st")
             nc.vector.scalar_tensor_tensor(out=wt[:], in0=e[t][:], scalar=1.0, in1=ub[:], op0=ALU.mult, op1=ALU.mult,
                                            accum_out=st[:])
-            si = eight.tile([P, 1], F32, name="si")
-            nc.vector.reciprocal(out=si[:], in_=st[:])
             w[t] = wt
+            rsum[t] = st
+
+        def row_inv(t):
+            si = eight.tile([P, 1], F32, name="si")
+            nc.vector.reciprocal(out=si[:], in_=rsum[t][:])
             sinv[t] = si
 
         def row_scale(t):
@@ -313,6 +343,7 @@ def tile_sinkhorndoublystochastictokenmixer_x1_kernel(tc, q, k, v, pos, g, out_0
 
         for t in range(3):
             col_norm(t)
+            row_inv(t)
             row_scale(t)
             if t < 2:
                 turn_mix(t)
@@ -322,8 +353,10 @@ def tile_sinkhorndoublystochastictokenmixer_x1_kernel(tc, q, k, v, pos, g, out_0
                 turn_mix(t + 2)
             if t + 3 < NT:
                 col_norm(t + 3)
-                row_scale(t + 3)
             quant_c(t)
+            if t + 3 < NT:
+                row_inv(t + 3)
+                row_scale(t + 3)
             if t < NT - 1:
                 mix(t)
                 leave(t)

@@ -11,366 +11,407 @@ U8 = mybir.dt.uint8
 FP8X4 = mybir.dt.float8_e4m3fn_x4
 ALU = mybir.AluOpType
 ACT = mybir.ActivationFunctionType
+AX = mybir.AxisListType
 
 S = 1024
 D = 512
 P = 128
-NT = 8
-ALPHA = 1.5 / (D ** 0.5)
+PACK = 4
+K_PASS = P * PACK
+GROUPS = S // K_PASS
+TILES = S // P
+BANK = 512
 
+SCORE_SCALE = 1.5 / D**0.5
 SHIFT = 40.0
-GROW = float(2 ** 56)
+GROW = float(2**56)
+GAIN_SCALE = S / S**0.5
 
-FLOPS = 2 * 2 * S * S * D
+FLOPS = 2 * (2 * S * S * D)
 
 
 def tile_sinkhorndoublystochastictokenmixer_x1_kernel(tc, q, k, v, pos, g, out_0, out_1, out_2):
     nc = tc.nc
     with ExitStack() as ctx:
-        one = ctx.enter_context(tc.tile_pool(name="one", bufs=1))
-        eight = ctx.enter_context(tc.tile_pool(name="eight", bufs=8))
-        three = ctx.enter_context(tc.tile_pool(name="three", bufs=3))
-        psl = ctx.enter_context(tc.psum_pool(name="psl", bufs=4))
-        pst = ctx.enter_context(tc.psum_pool(name="pst", bufs=2))
-        psa = ctx.enter_context(tc.psum_pool(name="psa", bufs=2))
+        keep = ctx.enter_context(tc.tile_pool(name="keep", bufs=1))
+        per_tile = ctx.enter_context(tc.tile_pool(name="per_tile", bufs=TILES))
+        ring = ctx.enter_context(tc.tile_pool(name="ring", bufs=3))
+        ps_main = ctx.enter_context(tc.psum_pool(name="ps_main", bufs=4))
+        ps_turn = ctx.enter_context(tc.psum_pool(name="ps_turn", bufs=2))
+        ps_sum = ctx.enter_context(tc.psum_pool(name="ps_sum", bufs=2))
         ctx.enter_context(tc.manual_schedule())
 
-        k_sb = [one.tile([P, 4, D], BF16, name="k_sb%d" % i, align_bytes=64) for i in range(2)]
-        q_sb = [one.tile([P, 4, D], BF16, name="q_sb%d" % i, align_bytes=64) for i in range(2)]
-        v_sb = [one.tile([P, 4, D], BF16, name="v_sb%d" % i, align_bytes=64) for i in range(2)]
-        pos_sb = [eight.tile([P, S], BF16, name="pos_sb", align_bytes=64) for i in range(NT)]
-        g_sb = one.tile([P, 2, 4], BF16, name="g_sb")
-        kv = k[0, :, :].rearrange("(g p t) d -> g p t d", g=2, t=4)
-        qv = q[0, :, :].rearrange("(g p t) d -> g p t d", g=2, t=4)
-        vv = v[0, :, :].rearrange("(g p t) d -> g p t d", g=2, t=4)
-        posv = pos.rearrange("(g p t) j -> g p t j", g=2, t=4)
+        rows = "(g p t) d -> g p t d"
+        q_hbm = q[0, :, :].rearrange(rows, g=GROUPS, t=PACK)
+        k_hbm = k[0, :, :].rearrange(rows, g=GROUPS, t=PACK)
+        v_hbm = v[0, :, :].rearrange(rows, g=GROUPS, t=PACK)
+        pos_hbm = pos.rearrange(rows, g=GROUPS, t=PACK)
+        out_hbm = out_0[0, :, :].rearrange(rows, g=GROUPS, t=PACK)
 
-        def load(dst, src, gi, lo, hi):
-            nc.sync.dma_start(out=dst[gi][:, lo:hi, :], in_=src[gi, :, lo:hi, :])
+        q_raw = [keep.tile([P, PACK, D], BF16, name="q_raw%d" % i, align_bytes=64) for i in range(GROUPS)]
+        k_raw = [keep.tile([P, PACK, D], BF16, name="k_raw%d" % i, align_bytes=64) for i in range(GROUPS)]
+        v_raw = [keep.tile([P, PACK, D], BF16, name="v_raw%d" % i, align_bytes=64) for i in range(GROUPS)]
+        pos_sb = [per_tile.tile([P, S], BF16, name="pos_sb", align_bytes=64) for i in range(TILES)]
+        g_sb = keep.tile([P, TILES], BF16, name="g_sb")
 
-        def load_pos(t):
-            nc.sync.dma_start(out=pos_sb[t][:], in_=posv[t // 4, :, t % 4, :])
+        def load(raw, hbm, grp, lo, hi):
+            nc.sync.dma_start(out=raw[grp][:, lo:hi, :], in_=hbm[grp, :, lo:hi, :])
 
-        load(q_sb, qv, 0, 0, 2)
-        load(k_sb, kv, 0, 0, 2)
-        load(k_sb, kv, 0, 2, 4)
-        load(k_sb, kv, 1, 0, 2)
-        load(k_sb, kv, 1, 2, 4)
+        def load_pos(n):
+            nc.sync.dma_start(out=pos_sb[n][:], in_=pos_hbm[n // PACK, :, n % PACK, :])
+
+        load(q_raw, q_hbm, 0, 0, 2)
+        load(k_raw, k_hbm, 0, 0, 2)
+        load(k_raw, k_hbm, 0, 2, 4)
+        load(k_raw, k_hbm, 1, 0, 2)
+        load(k_raw, k_hbm, 1, 2, 4)
         load_pos(0)
         load_pos(1)
-        load(q_sb, qv, 0, 2, 4)
+        load(q_raw, q_hbm, 0, 2, 4)
         load_pos(2)
         load_pos(3)
-        load(q_sb, qv, 1, 0, 4)
-        load_pos(4)
-        load_pos(5)
-        load_pos(6)
-        load_pos(7)
-        load(v_sb, vv, 0, 0, 4)
-        load(v_sb, vv, 1, 0, 4)
-        nc.sync.dma_start(out=g_sb[:], in_=g.rearrange("(g p t) -> p g t", g=2, t=4))
+        load(q_raw, q_hbm, 1, 0, 4)
+        for n in range(4, TILES):
+            load_pos(n)
+        load(v_raw, v_hbm, 0, 0, 4)
+        load(v_raw, v_hbm, 1, 0, 4)
+        nc.sync.dma_start(
+            out=g_sb[:].rearrange("p (g t) -> p g t", t=PACK),
+            in_=g.rearrange("(g p t) -> p g t", g=GROUPS, t=PACK),
+        )
 
-        ident = one.tile([P, P], F32, name="ident")
+        ident = keep.tile([P, P], F32, name="ident")
         make_identity(nc, ident[:])
 
-        k_gr = [one.tile([P, 512, 4], BF16, name="k_gr%d" % i, align_bytes=64) for i in range(2)]
-        k_c = [one.tile([P, 512], U32, name="k_c%d" % i, align_bytes=64) for i in range(2)]
-        k_s = [one.tile([P, 512], U8, name="k_s%d" % i, align_bytes=64) for i in range(2)]
-        q_gr = [one.tile([P, 256, 4], BF16, name="q_gr%d" % i, align_bytes=64) for i in range(4)]
-        q_c = [one.tile([P, 256], U32, name="q_c%d" % i, align_bytes=64) for i in range(4)]
-        q_s = [one.tile([P, 256], U8, name="q_s%d" % i, align_bytes=64) for i in range(4)]
-        v_gr = [one.tile([P, D, 4], BF16, name="v_gr%d" % i, align_bytes=64) for i in range(2)]
-        v_c = [one.tile([P, D], U32, name="v_c%d" % i, align_bytes=64) for i in range(2)]
-        v_s = [one.tile([P, D], U8, name="v_s%d" % i, align_bytes=64) for i in range(2)]
+        def mx_tiles(label, width):
+            woven = keep.tile([P, width, PACK], BF16, name=label + "_woven", align_bytes=64)
+            codes = keep.tile([P, width], U32, name=label + "_codes", align_bytes=64)
+            scales = keep.tile([P, width], U8, name=label + "_scales", align_bytes=64)
+            return woven, codes, scales
 
-        def turn_pair(src, t0, pool=pst, name="tp"):
-            bank = pool.tile([P, 2, 256], F32, name=name)
-            for tt in range(2):
-                words = src[:, t0 + tt, :].bitcast(F32)
+        def quantize(operand, lo, hi):
+            woven, codes, scales = operand
+            nc.vector.quantize_mx(
+                out=codes[:, lo:hi].bitcast(FP8X4),
+                scales=scales[:, lo:hi],
+                in_=woven[:, lo:hi, :].rearrange("p c t -> p (c t)"),
+            )
+
+        k_mx = [mx_tiles("k%d" % i, K_PASS) for i in range(GROUPS)]
+        q_mx = [mx_tiles("q%d" % i, 2 * P) for i in range(TILES // 2)]
+        v_mx = [mx_tiles("v%d" % i, D) for i in range(GROUPS)]
+        o_mx = [mx_tiles("o%d" % i, D) for i in range(GROUPS)]
+
+        def turn_pair(raw, t, pool, label):
+            bank = pool.tile([P, 2, 2 * P], F32, name=label)
+            for s in range(2):
+                words = raw[:, t + s, :].bitcast(F32)
                 for u in range(2):
-                    nc.tensor.transpose(bank[:, u, tt * P:(tt + 1) * P], words[:, u:256:2], ident[:])
+                    nc.tensor.transpose(bank[:, u, s * P : (s + 1) * P], words[:, u : D // 2 : 2], ident[:])
             return bank
 
-        def move_words(copy, bank, dst):
-            copy(out=dst.rearrange("p r j -> p (r j)").bitcast(F32).rearrange("p (r u) -> p r u", u=2),
-                 in_=bank[:].rearrange("p u r -> p r u"))
+        def weave_words(copy, bank, woven):
+            copy(
+                out=woven.rearrange("p c t -> p (c t)").bitcast(F32).rearrange("p (c u) -> p c u", u=2),
+                in_=bank[:].rearrange("p u c -> p c u"),
+            )
 
-        def quant(gr, codes, scales):
-            nc.vector.quantize_mx(out=codes[:].bitcast(FP8X4), scales=scales[:],
-                                  in_=gr[:].rearrange("p r j -> p (r j)"))
+        def turn_q(pair, copy):
+            bank = turn_pair(q_raw[pair // 2], 2 * (pair % 2), ps_turn, "turned")
+            weave_words(copy, bank, q_mx[pair][0][:])
 
-        def q_turn(h, copy=nc.scalar.copy, **where):
-            bank = turn_pair(q_sb[h // 2], (h % 2) * 2, **where)
-            move_words(copy, bank, q_gr[h][:])
+        def turn_k(grp, half, copy, pool, label):
+            bank = turn_pair(k_raw[grp], 2 * half, pool, label)
+            weave_words(copy, bank, k_mx[grp][0][:, half * 2 * P : (half + 1) * 2 * P, :])
 
-        def k_turn(gi, half, copy, **where):
-            bank = turn_pair(k_sb[gi], 2 * half, **where)
-            move_words(copy, bank, k_gr[gi][:, half * 256:(half + 1) * 256, :])
+        def weave_v(grp, half):
+            cols = slice(half * D // 2, (half + 1) * D // 2)
+            dst = v_mx[grp][0][:, cols, :]
+            src = v_raw[grp][:, :, cols].rearrange("p t d -> p d t")
+            if grp == 0:
+                nc.gpsimd.tensor_scalar(out=dst, in0=src, scalar1=1.0, scalar2=0.0, op0=ALU.mult, op1=ALU.add)
+            else:
+                nc.scalar.copy(out=dst, in_=src)
 
-        def k_quant(gi, half):
-            cols = slice(half * 256, (half + 1) * 256)
-            nc.vector.quantize_mx(out=k_c[gi][:, cols].bitcast(FP8X4), scales=k_s[gi][:, cols],
-                                  in_=k_gr[gi][:, cols, :].rearrange("p r j -> p (r j)"))
-
-        lp = {}
-
-        def scores(t, half=(0, 1)):
-            h = t // 2
-            cols = slice((t % 2) * P, (t % 2 + 1) * P)
-            for gj in half:
-                bank = psl.tile([P, 512], F32, name="lp")
-                nc.tensor.matmul_mx(out=bank[:], lhsT=q_c[h][:, cols].bitcast(FP8X4), lhsT_scale=q_s[h][:, cols],
-                                    rhs=k_c[gj][:].bitcast(FP8X4), rhs_scale=k_s[gj][:], start=True, stop=True)
-                lp[t, gj] = bank
-
+        score_bank = {}
         neg_l = {}
-        neg_m = {}
-        e = {}
-        row = {}
-        rinv = {}
+        shift = {}
+        weight = {}
+        row_sum = {}
+        row_inv = {}
 
-        def add_pos(t, halves=(0, 1)):
-            if t not in neg_l:
-                nl = three.tile([P, S], F32, name="nl")
-                neg_l[t] = nl
-            nl = neg_l[t]
-            for gj in halves:
-                half = slice(gj * 512, (gj + 1) * 512)
-                nc.vector.scalar_tensor_tensor(
-                    out=nl[:, half].rearrange("p (t a) -> p t a", t=4),
-                    in0=lp[t, gj][:].rearrange("p (t a) -> p t a", t=4),
-                    scalar=-ALPHA,
-                    in1=pos_sb[t][:, half].rearrange("p (a t) -> p t a", t=4),
-                    op0=ALU.mult, op1=ALU.subtract)
+        def scores(n, grps):
+            cols = slice((n % 2) * P, (n % 2 + 1) * P)
+            for grp in grps:
+                bank = ps_main.tile([P, BANK], F32, name="main")
+                nc.tensor.matmul_mx(
+                    out=bank[:],
+                    lhsT=q_mx[n // 2][1][:, cols].bitcast(FP8X4),
+                    lhsT_scale=q_mx[n // 2][2][:, cols],
+                    rhs=k_mx[grp][1][:].bitcast(FP8X4),
+                    rhs_scale=k_mx[grp][2][:],
+                    start=True,
+                    stop=True,
+                )
+                score_bank[n, grp] = bank
 
-        def row_max(t):
-            junk = three.tile([P, S], F32, name="junk")
-            nm = eight.tile([P, 1], F32, name="nm")
-            nc.vector.tensor_scalar(out=junk[:], in0=neg_l[t][:], scalar1=SHIFT, scalar2=None,
-                                    op0=ALU.add, op1=ALU.min, accum_out=nm[:])
-            neg_m[t] = nm
+        def add_pos(n, grp):
+            if n not in neg_l:
+                nl = ring.tile([P, S], F32, name="nl")
+                neg_l[n] = nl
+            half = slice(grp * BANK, (grp + 1) * BANK)
+            nc.vector.scalar_tensor_tensor(
+                out=neg_l[n][:, half].rearrange("p (t a) -> p t a", t=PACK),
+                in0=score_bank[n, grp][:].rearrange("p (t a) -> p t a", t=PACK),
+                scalar=-SCORE_SCALE,
+                in1=pos_sb[n][:, half].rearrange("p (a t) -> p t a", t=PACK),
+                op0=ALU.mult,
+                op1=ALU.subtract,
+            )
 
-        def expo(t):
-            et = eight.tile([P, S], F32, name="et")
-            rt = eight.tile([P, 1], F32, name="rt")
-            nc.scalar.activation(out=et[:], in_=neg_l[t][:], func=ACT.Exp, bias=neg_m[t][:], scale=-1.0,
-                                 accum_out=rt[:])
-            e[t] = et
-            row[t] = rt
+        def row_max(n):
+            spare = ring.tile([P, S], F32, name="spare")
+            sh = per_tile.tile([P, 1], F32, name="sh")
+            nc.vector.tensor_scalar(
+                out=spare[:], in0=neg_l[n][:], scalar1=SHIFT, scalar2=None, op0=ALU.add, op1=ALU.min, accum_out=sh[:]
+            )
+            shift[n] = sh
 
-        def row_recip(t):
-            ri = eight.tile([P, 1], F32, name="ri")
-            nc.vector.reciprocal(out=ri[:], in_=row[t][:])
-            rinv[t] = ri
+        def exponentials(n):
+            et = per_tile.tile([P, S], F32, name="et")
+            rt = per_tile.tile([P, 1], F32, name="rt")
+            nc.scalar.activation(
+                out=et[:], in_=neg_l[n][:], func=ACT.Exp, bias=shift[n][:], scale=-1.0, accum_out=rt[:]
+            )
+            weight[n] = et
+            row_sum[n] = rt
 
-        def row_norm(t):
-            ri = rinv[t]
-            eng = nc.vector if t >= NT - 2 else nc.gpsimd
-            pieces = 2 if t == NT - 1 else 1
-            for n in range(pieces):
-                part = slice(n * S // pieces, (n + 1) * S // pieces)
-                eng.tensor_scalar(out=e[t][:, part], in0=e[t][:, part], scalar1=GROW, scalar2=ri[:],
-                                  op0=ALU.mult, op1=ALU.mult)
+        def row_reciprocal(n):
+            ri = per_tile.tile([P, 1], F32, name="ri")
+            nc.vector.reciprocal(out=ri[:], in_=row_sum[n][:])
+            row_inv[n] = ri
 
-        acc = [psa.tile([P, 4, P], F32, name="acc") for i in range(2)]
+        def row_normalise(n, engine, pieces):
+            for i in range(pieces):
+                cols = slice(i * S // pieces, (i + 1) * S // pieces)
+                engine.tensor_scalar(
+                    out=weight[n][:, cols],
+                    in0=weight[n][:, cols],
+                    scalar1=GROW,
+                    scalar2=row_inv[n][:],
+                    op0=ALU.mult,
+                    op1=ALU.mult,
+                )
 
-        def col_add(t):
-            for gj in range(2):
-                for tj in range(4):
-                    c0 = (gj * 4 + tj) * P
-                    nc.tensor.matmul(out=acc[gj][:, tj, :], lhsT=e[t][:, c0:c0 + P], rhs=ident[:],
-                                     start=(t == 0 and tj == 0), stop=(t == NT - 1 and tj == 3), is_transpose=True)
+        col_bank = [ps_sum.tile([P, PACK, P], F32, name="sum") for i in range(GROUPS)]
 
-        q_turn(0, nc.vector.tensor_copy)
-        k_turn(0, 0, nc.scalar.copy)
-        quant(q_gr[0], q_c[0], q_s[0])
-        k_turn(0, 1, nc.vector.tensor_copy, pool=psl, name="lp")
-        k_quant(0, 0)
-        k_quant(0, 1)
-        k_turn(1, 0, nc.scalar.copy, pool=psl, name="lp")
-        k_turn(1, 1, nc.scalar.copy)
+        def add_columns(n):
+            for grp in range(GROUPS):
+                for t in range(PACK):
+                    c0 = (grp * PACK + t) * P
+                    nc.tensor.matmul(
+                        out=col_bank[grp][:, t, :],
+                        lhsT=weight[n][:, c0 : c0 + P],
+                        rhs=ident[:],
+                        start=(n == 0 and t == 0),
+                        stop=(n == TILES - 1 and t == PACK - 1),
+                        is_transpose=True,
+                    )
+
+        turn_q(0, nc.vector.tensor_copy)
+        turn_k(0, 0, nc.scalar.copy, ps_turn, "turned")
+        quantize(q_mx[0], 0, 2 * P)
+        turn_k(0, 1, nc.vector.tensor_copy, ps_main, "main")
+        quantize(k_mx[0], 0, 2 * P)
+        quantize(k_mx[0], 2 * P, K_PASS)
+        turn_k(1, 0, nc.scalar.copy, ps_main, "main")
+        turn_k(1, 1, nc.scalar.copy, ps_turn, "turned")
         scores(0, (0,))
         scores(1, (0,))
-        q_turn(1)
-        add_pos(0, (0,))
-        k_quant(1, 0)
-        k_quant(1, 1)
-        add_pos(1, (0,))
+        turn_q(1, nc.scalar.copy)
+        add_pos(0, 0)
+        quantize(k_mx[1], 0, K_PASS)
+        add_pos(1, 0)
         scores(0, (1,))
         scores(1, (1,))
 
-        def v_move(gi, part, copy):
-            cols = slice(part * 256, (part + 1) * 256)
-            copy(out=v_gr[gi][:, cols, :], in_=v_sb[gi][:, :, cols].rearrange("p t d -> p d t"))
+        for n in range(TILES):
+            if n < 2:
+                turn_q(n + 2, nc.scalar.copy)
+            add_pos(n, 1)
+            if 0 < n < TILES - 1:
+                add_pos(n + 1, 0)
+            row_max(n)
+            exponentials(n)
+            if n < 3:
+                quantize(q_mx[n + 1], 0, 2 * P)
+            if n > 0:
+                row_reciprocal(n - 1)
+                row_normalise(n - 1, nc.vector if n == TILES - 1 else nc.gpsimd, 1)
+            if n + 2 < TILES:
+                scores(n + 2, (0, 1))
+            if n >= 2:
+                add_columns(n - 2)
+            if n == 3 or n == 5:
+                weave_v(0, n // 2 - 1)
+        quantize(v_mx[0], 0, D)
+        gain = keep.tile([P, TILES], F32, name="gain")
+        nc.vector.tensor_scalar(out=gain[:], in0=g_sb[:], scalar1=GAIN_SCALE, scalar2=None, op0=ALU.mult)
+        row_reciprocal(TILES - 1)
+        row_normalise(TILES - 1, nc.vector, 2)
+        add_columns(TILES - 2)
+        add_columns(TILES - 1)
+        weave_v(1, 0)
+        weave_v(1, 1)
 
-        for t in range(NT):
-            if t == 1 or t == 3:
-                q_turn(t // 2 + 2)
-            add_pos(t, (1,))
-            if t > 0 and t + 1 < NT:
-                add_pos(t + 1, (0,))
-            row_max(t)
-            expo(t)
-            if t % 2 == 0 and t < 6:
-                h = t // 2 + 1
-                quant(q_gr[h], q_c[h], q_s[h])
-            if t > 0:
-                row_recip(t - 1)
-                row_norm(t - 1)
-            if t + 2 < NT:
-                scores(t + 2)
-            if t > 0:
-                col_add(t - 1)
-            if t == 3 or t == 5:
-                v_move(0, (t - 3) // 2, nc.scalar.copy)
-        quant(v_gr[0], v_c[0], v_s[0])
-        g32 = one.tile([P, 8], F32, name="g32")
-        nc.vector.tensor_scalar(out=g32[:], in0=g_sb[:].rearrange("p g t -> p (g t)"), scalar1=S / (S ** 0.5),
-                                scalar2=None, op0=ALU.mult)
-        row_recip(NT - 1)
-        row_norm(NT - 1)
-        col_add(NT - 1)
-        v_move(1, 0, nc.scalar.copy)
-        v_move(1, 1, nc.scalar.copy)
+        col_sum = keep.tile([P, TILES], F32, name="col_sum")
+        u = keep.tile([P, TILES], F32, name="u")
+        u_row = keep.tile([P, S], F32, name="u_row")
+        for grp in range(GROUPS):
+            cols = slice(grp * PACK, (grp + 1) * PACK)
+            nc.vector.tensor_reduce(out=col_sum[:, cols], in_=col_bank[grp][:], axis=AX.X, op=ALU.add)
+            nc.vector.reciprocal(out=u[:, cols], in_=col_sum[:, cols])
+            spread = ps_turn.tile([P, PACK, P], F32, name="turned")
+            for t in range(PACK):
+                b = grp * PACK + t
+                nc.tensor.transpose(spread[:, t, :], u[:, b : b + 1].to_broadcast([P, P]), ident[:])
+            nc.scalar.copy(
+                out=u_row[:, grp * BANK : (grp + 1) * BANK], in_=spread[:].rearrange("p t a -> p (t a)")
+            )
+        quantize(v_mx[1], 0, D)
 
-        u = one.tile([P, 8], F32, name="u")
-        csum = one.tile([P, 8], F32, name="csum")
-        ub = one.tile([P, S], F32, name="ub")
-        for gj in range(2):
-            cols = slice(gj * 4, (gj + 1) * 4)
-            nc.vector.tensor_reduce(out=csum[:, cols], in_=acc[gj][:], axis=mybir.AxisListType.X, op=ALU.add)
-            nc.vector.reciprocal(out=u[:, cols], in_=csum[:, cols])
-            if gj == 1:
-                quant(v_gr[1], v_c[1], v_s[1])
-            bank = pst.tile([P, 512], F32, name="tp")
-            for tj in range(4):
-                b = gj * 4 + tj
-                nc.tensor.transpose(bank[:, tj * P:(tj + 1) * P], u[:, b:b + 1].to_broadcast([P, P]), ident[:])
-            (nc.vector.tensor_copy if gj else nc.scalar.copy)(out=ub[:, gj * 512:(gj + 1) * 512], in_=bank[:])
+        mixed = {}
+        mix_sum = {}
+        mix_inv = {}
+        deviation = {}
+        turned = {}
+        c_woven = {}
+        c_codes = {}
+        c_scales = {}
 
-        w = {}
-        sinv = {}
-        rsum = {}
-        x = {}
-        xt = {}
-        c_gr = {}
-        c_c = {}
-        c_s = {}
-        o32 = {}
-        o_ps = {}
+        def scale_columns(n):
+            wt = ring.tile([P, S], F32, name="wt")
+            st = per_tile.tile([P, 1], F32, name="st")
+            nc.vector.scalar_tensor_tensor(
+                out=wt[:],
+                in0=weight[n][:],
+                scalar=1.0,
+                in1=u_row[:],
+                op0=ALU.mult,
+                op1=ALU.mult,
+                accum_out=st[:],
+            )
+            mixed[n] = wt
+            mix_sum[n] = st
 
-        def col_norm(t):
-            wt = three.tile([P, S], F32, name="wt")
-            st = eight.tile([P, 1], F32, name="st")
-            nc.vector.scalar_tensor_tensor(out=wt[:], in0=e[t][:], scalar=1.0, in1=ub[:], op0=ALU.mult, op1=ALU.mult,
-                                           accum_out=st[:])
-            w[t] = wt
-            rsum[t] = st
+        def scale_rows(n):
+            si = per_tile.tile([P, 1], F32, name="si")
+            nc.vector.reciprocal(out=si[:], in_=mix_sum[n][:])
+            dv = ring.tile([P, S], F32, name="dv")
+            nc.scalar.activation(out=dv[:], in_=mixed[n][:], func=ACT.Copy, bias=-1.0 / S, scale=si[:])
+            deviation[n] = dv
 
-        def row_inv(t):
-            si = eight.tile([P, 1], F32, name="si")
-            nc.vector.reciprocal(out=si[:], in_=rsum[t][:])
-            sinv[t] = si
+        def turn_mix(n):
+            for grp in range(GROUPS):
+                bank = ps_main.tile([P, PACK, P], F32, name="main")
+                for t in range(PACK):
+                    c0 = (grp * PACK + t) * P
+                    nc.tensor.transpose(bank[:, t, :], deviation[n][:, c0 : c0 + P], ident[:])
+                turned[n, grp] = bank
 
-        def row_scale(t):
-            xx = three.tile([P, S], F32, name="xx")
-            nc.scalar.activation(out=xx[:], in_=w[t][:], func=ACT.Copy, bias=-1.0 / S, scale=sinv[t][:])
-            x[t] = xx
-
-        def turn_mix(t):
-            for gj in range(2):
-                bank = psl.tile([P, 4, P], F32, name="lp")
-                for tj in range(4):
-                    c0 = (gj * 4 + tj) * P
-                    nc.tensor.transpose(bank[:, tj, :], x[t][:, c0:c0 + P], ident[:])
-                xt[t, gj] = bank
-
-        def gain(t):
-            cg = three.tile([P, 2, P, 4], BF16, name="cg", align_bytes=64)
-            for gj in range(2):
+        def apply_gain(n):
+            cw = ring.tile([P, GROUPS, P, PACK], BF16, name="cw", align_bytes=64)
+            for grp in range(GROUPS):
+                gain_cols = gain[:, grp * PACK : (grp + 1) * PACK]
                 nc.vector.tensor_tensor(
-                    out=cg[:, gj, :, :],
-                    in0=xt[t, gj][:].rearrange("p t i -> p i t"),
-                    in1=g32[:, gj * 4:(gj + 1) * 4].unsqueeze(1).to_broadcast([P, P, 4]),
-                    op=ALU.mult)
-            c_gr[t] = cg
+                    out=cw[:, grp, :, :],
+                    in0=turned[n, grp][:].rearrange("p t i -> p i t"),
+                    in1=gain_cols.unsqueeze(1).to_broadcast([P, P, PACK]),
+                    op=ALU.mult,
+                )
+            c_woven[n] = cw
 
-        def quant_c(t):
-            cc = three.tile([P, 256], U32, name="cc", align_bytes=64)
-            cs = three.tile([P, 256], U8, name="cs", align_bytes=64)
-            nc.vector.quantize_mx(out=cc[:].bitcast(FP8X4), scales=cs[:],
-                                  in_=c_gr[t][:].rearrange("p g i t -> p (g i t)"))
-            c_c[t] = cc
-            c_s[t] = cs
+        def quantize_c(n):
+            cc = ring.tile([P, GROUPS * P], U32, name="cc", align_bytes=64)
+            cs = ring.tile([P, GROUPS * P], U8, name="cs", align_bytes=64)
+            nc.vector.quantize_mx(
+                out=cc[:].bitcast(FP8X4), scales=cs[:], in_=c_woven[n][:].rearrange("p g i t -> p (g i t)")
+            )
+            c_codes[n] = cc
+            c_scales[n] = cs
 
-        def mix_part(t, bank, lo, hi):
-            for gj in range(2):
-                cols = slice(gj * P, (gj + 1) * P)
-                nc.tensor.matmul_mx(out=bank[:, 0:hi - lo], lhsT=c_c[t][:, cols].bitcast(FP8X4),
-                                    lhsT_scale=c_s[t][:, cols],
-                                    rhs=v_c[gj][:, lo:hi].bitcast(FP8X4), rhs_scale=v_s[gj][:, lo:hi],
-                                    start=(gj == 0), stop=(gj == 1))
+        def mix(n, bank, lo, hi):
+            for grp in range(GROUPS):
+                cols = slice(grp * P, (grp + 1) * P)
+                nc.tensor.matmul_mx(
+                    out=bank[:, 0 : hi - lo],
+                    lhsT=c_codes[n][:, cols].bitcast(FP8X4),
+                    lhsT_scale=c_scales[n][:, cols],
+                    rhs=v_mx[grp][1][:, lo:hi].bitcast(FP8X4),
+                    rhs_scale=v_mx[grp][2][:, lo:hi],
+                    start=(grp == 0),
+                    stop=(grp == GROUPS - 1),
+                )
 
-        def mix(t):
-            bank = psa.tile([P, 512], F32, name="acc")
-            mix_part(t, bank, 0, D)
-            o_ps[t] = bank
+        out_sb = [keep.tile([P, PACK, D], F32, name="out_sb%d" % i) for i in range(GROUPS)]
 
-        outv = out_0[0, :, :].rearrange("(g p t) d -> g p t d", g=2, t=4)
-        o_sb = [one.tile([P, 4, D], F32, name="o_sb%d" % i) for i in range(2)]
-        o_gr = [one.tile([P, D, 4], BF16, name="o_gr%d" % i, align_bytes=64) for i in range(2)]
-        o_c = [one.tile([P, D], U32, name="o_c%d" % i, align_bytes=64) for i in range(2)]
-        o_s = [one.tile([P, D], U8, name="o_s%d" % i, align_bytes=64) for i in range(2)]
+        def store_rows(n):
+            grp, t = n // PACK, n % PACK
+            nc.sync.dma_start(out=out_hbm[grp, :, t, :], in_=out_sb[grp][:, t, :])
 
-        def leave(t):
-            nc.scalar.copy(out=o_sb[t // 4][:, t % 4, :], in_=o_ps[t][:])
-            nc.sync.dma_start(out=outv[t // 4, :, t % 4, :], in_=o_sb[t // 4][:, t % 4, :])
+        def weave_out(grp, lo, hi, copy):
+            copy(out=o_mx[grp][0][:, lo:hi, :], in_=out_sb[grp][:, :, lo:hi].rearrange("p t d -> p d t"))
 
-        def group_move(gi, lo, hi, copy):
-            cols = slice(lo, hi)
-            copy(out=o_gr[gi][:, cols, :], in_=o_sb[gi][:, :, cols].rearrange("p t d -> p d t"))
+        def store_planes(grp):
+            codes, scales = o_mx[grp][1], o_mx[grp][2]
+            nc.sync.dma_start(
+                out=out_1[grp, :, :, :].rearrange("p m t -> p (m t)").bitcast(I32), in_=codes[:].bitcast(I32)
+            )
+            for quad in range(4):
+                nc.sync.dma_start(
+                    out=out_2[grp, 4 * quad : 4 * quad + 4, :].bitcast(I32),
+                    in_=scales[32 * quad : 32 * quad + 4, :].bitcast(I32),
+                )
 
-        def group_out(gi):
-            for part in range(2):
-                cols = slice(part * 256, (part + 1) * 256)
-                nc.vector.quantize_mx(out=o_c[gi][:, cols].bitcast(FP8X4), scales=o_s[gi][:, cols],
-                                      in_=o_gr[gi][:, cols, :].rearrange("p m t -> p (m t)"))
-            nc.sync.dma_start(out=out_1[gi, :, :, :].rearrange("p m t -> p (m t)").bitcast(I32),
-                              in_=o_c[gi][:].bitcast(I32))
-            for qd in range(4):
-                nc.sync.dma_start(out=out_2[gi, 4 * qd:4 * qd + 4, :].bitcast(I32),
-                                  in_=o_s[gi][32 * qd:32 * qd + 4, :].bitcast(I32))
+        LEAD = 3
+        for n in range(LEAD):
+            scale_columns(n)
+            scale_rows(n)
+            if n < 2:
+                turn_mix(n)
+        for n in range(TILES):
+            apply_gain(n)
+            if n == 0:
+                turn_mix(2)
+            if n + LEAD < TILES:
+                scale_columns(n + LEAD)
+            quantize_c(n)
+            if n + LEAD < TILES:
+                scale_rows(n + LEAD)
+            if 0 < n < TILES - 2:
+                turn_mix(n + 2)
+            if n < TILES - 1:
+                bank = ps_sum.tile([P, BANK], F32, name="sum")
+                mix(n, bank, 0, D)
+                nc.scalar.copy(out=out_sb[n // PACK][:, n % PACK, :], in_=bank[:])
+                store_rows(n)
+            if n == 4 or n == 5:
+                weave_out(0, (n - 4) * D // 2, (n - 3) * D // 2, nc.scalar.copy)
 
-        for t in range(3):
-            col_norm(t)
-            row_inv(t)
-            row_scale(t)
-            if t < 2:
-                turn_mix(t)
-        for t in range(NT):
-            gain(t)
-            if t + 2 < NT:
-                turn_mix(t + 2)
-            if t + 3 < NT:
-                col_norm(t + 3)
-            quant_c(t)
-            if t + 3 < NT:
-                row_inv(t + 3)
-                row_scale(t + 3)
-            if t < NT - 1:
-                mix(t)
-                leave(t)
-            if t == 4 or t == 5:
-                group_move(0, (t - 4) * 256, (t - 3) * 256, nc.scalar.copy)
-        last = NT - 1
-        low = psa.tile([P, 512], F32, name="acc")
-        high = pst.tile([P, 512], F32, name="tp")
-        mix_part(last, low, 0, 256)
-        mix_part(last, high, 256, 512)
-        group_out(0)
-        nc.vector.tensor_copy(out=o_sb[1][:, 3, 0:256], in_=low[:, 0:256])
-        nc.scalar.copy(out=o_sb[1][:, 3, 256:512], in_=high[:, 0:256])
-        nc.sync.dma_start(out=outv[1, :, 3, :], in_=o_sb[1][:, 3, :])
-        group_move(1, 0, 320, nc.vector.tensor_copy)
-        group_move(1, 320, 512, nc.scalar.copy)
-        group_out(1)
+        last = TILES - 1
+        half = D // 2
+        low = ps_sum.tile([P, BANK], F32, name="sum")
+        high = ps_turn.tile([P, BANK], F32, name="turned")
+        mix(last, low, 0, half)
+        mix(last, high, half, D)
+        quantize(o_mx[0], 0, D)
+        store_planes(0)
+        nc.vector.tensor_copy(out=out_sb[1][:, PACK - 1, 0:half], in_=low[:, 0:half])
+        nc.scalar.copy(out=out_sb[1][:, PACK - 1, half:D], in_=high[:, 0:half])
+        store_rows(last)
+        VECTOR_COLS = 320
+        weave_out(1, 0, VECTOR_COLS, nc.vector.tensor_copy)
+        weave_out(1, VECTOR_COLS, D, nc.scalar.copy)
+        quantize(o_mx[1], 0, half)
+        quantize(o_mx[1], half, D)
+        store_planes(1)

@@ -267,6 +267,7 @@ def tile_sinkhorndoublystochastictokenmixer_x1_kernel(tc, q, k, v, pos, g, out_0
         col_sum = keep.tile([P, TILES], F32, name="col_sum")
         u = keep.tile([P, TILES], F32, name="u")
         u_row = keep.tile([P, S], F32, name="u_row")
+        u_bank = []
         for grp in range(GROUPS):
             cols = slice(grp * PACK, (grp + 1) * PACK)
             nc.vector.tensor_reduce(out=col_sum[:, cols], in_=col_bank[grp][:], axis=AX.X, op=ALU.add)
@@ -275,10 +276,7 @@ def tile_sinkhorndoublystochastictokenmixer_x1_kernel(tc, q, k, v, pos, g, out_0
             for t in range(PACK):
                 b = grp * PACK + t
                 nc.tensor.transpose(spread[:, t, :], u[:, b : b + 1].to_broadcast([P, P]), ident[:])
-            nc.scalar.copy(
-                out=u_row[:, grp * BANK : (grp + 1) * BANK], in_=spread[:].rearrange("p t a -> p (t a)")
-            )
-        quantize(v_mx[1], 0, D)
+            u_bank.append(spread)
 
         mixed = {}
         mix_sum = {}
@@ -303,6 +301,28 @@ def tile_sinkhorndoublystochastictokenmixer_x1_kernel(tc, q, k, v, pos, g, out_0
             )
             mixed[n] = wt
             mix_sum[n] = st
+
+        def scale_columns_first():
+            wt = ring.tile([P, S], F32, name="wt")
+            parts = per_tile.tile([P, GROUPS], F32, name="parts")
+            for grp in range(GROUPS):
+                half = slice(grp * BANK, (grp + 1) * BANK)
+                spread = u_bank[grp][:].rearrange("p t a -> p (t a)")
+                nc.vector.scalar_tensor_tensor(
+                    out=wt[:, half],
+                    in0=weight[0][:, half],
+                    scalar=1.0,
+                    in1=spread,
+                    op0=ALU.mult,
+                    op1=ALU.mult,
+                    accum_out=parts[:, grp : grp + 1],
+                )
+                nc.scalar.copy(out=u_row[:, half], in_=spread)
+            quantize(v_mx[1], 0, D)
+            st = per_tile.tile([P, 1], F32, name="st")
+            nc.vector.tensor_tensor(out=st[:], in0=parts[:, 0:1], in1=parts[:, 1:2], op=ALU.add)
+            mixed[0] = wt
+            mix_sum[0] = st
 
         def scale_rows(n):
             si = per_tile.tile([P, 1], F32, name="si")
@@ -375,16 +395,22 @@ def tile_sinkhorndoublystochastictokenmixer_x1_kernel(tc, q, k, v, pos, g, out_0
 
         LEAD = 3
         for n in range(LEAD):
-            scale_columns(n)
+            if n == 0:
+                scale_columns_first()
+            else:
+                scale_columns(n)
             scale_rows(n)
             if n < 2:
                 turn_mix(n)
         for n in range(TILES):
-            apply_gain(n)
+            if n <= TILES - LEAD:
+                apply_gain(n)
             if n == 0:
                 turn_mix(2)
             if n + LEAD < TILES:
                 scale_columns(n + LEAD)
+            elif n + 1 < TILES:
+                apply_gain(n + 1)
             quantize_c(n)
             if n + LEAD < TILES:
                 scale_rows(n + LEAD)
@@ -395,8 +421,8 @@ def tile_sinkhorndoublystochastictokenmixer_x1_kernel(tc, q, k, v, pos, g, out_0
                 mix(n, bank, 0, D)
                 nc.scalar.copy(out=out_sb[n // PACK][:, n % PACK, :], in_=bank[:])
                 store_rows(n)
-            if n == 4 or n == 5:
-                weave_out(0, (n - 4) * D // 2, (n - 3) * D // 2, nc.scalar.copy)
+            if n == 3 or n == 4:
+                weave_out(0, (n - 3) * D // 2, (n - 2) * D // 2, nc.scalar.copy)
 
         last = TILES - 1
         half = D // 2
@@ -409,9 +435,8 @@ def tile_sinkhorndoublystochastictokenmixer_x1_kernel(tc, q, k, v, pos, g, out_0
         nc.vector.tensor_copy(out=out_sb[1][:, PACK - 1, 0:half], in_=low[:, 0:half])
         nc.scalar.copy(out=out_sb[1][:, PACK - 1, half:D], in_=high[:, 0:half])
         store_rows(last)
-        VECTOR_COLS = 320
-        weave_out(1, 0, VECTOR_COLS, nc.vector.tensor_copy)
-        weave_out(1, VECTOR_COLS, D, nc.scalar.copy)
+        weave_out(1, 0, half, nc.vector.tensor_copy)
+        weave_out(1, half, D, nc.scalar.copy)
         quantize(o_mx[1], 0, half)
         quantize(o_mx[1], half, D)
         store_planes(1)

from contextlib import ExitStack

import concourse.mybir as mybir
from concourse.masks import make_identity

F32 = mybir.dt.float32
BF16 = mybir.dt.bfloat16
U32 = mybir.dt.uint32
I32 = mybir.dt.int32
U8 = mybir.dt.uint8
FP8X4 = mybir.dt.float8_e4m3fn_x4
ALU = mybir.AluOpType
ACT = mybir.ActivationFunctionType
AX = mybir.AxisListType

S = 1024
D = 512
P = 128
PACK = 4
K_PASS = P * PACK
GROUPS = S // K_PASS
TILES = S // P
BANK = 512

SCORE_SCALE = 1.5 / D**0.5
SHIFT = 40.0
GROW = float(2**56)
GAIN_SCALE = S / S**0.5

FLOPS = 2 * (2 * S * S * D)


def tile_sinkhorndoublystochastictokenmixer_x1_kernel(tc, q, k, v, pos, g, out_0, out_1, out_2):
    nc = tc.nc
    with ExitStack() as ctx:
        keep = ctx.enter_context(tc.tile_pool(name="keep", bufs=1))
        per_tile = ctx.enter_context(tc.tile_pool(name="per_tile", bufs=TILES))
        ring = ctx.enter_context(tc.tile_pool(name="ring", bufs=3))
        ps_main = ctx.enter_context(tc.psum_pool(name="ps_main", bufs=4))
        ps_turn = ctx.enter_context(tc.psum_pool(name="ps_turn", bufs=2))
        ps_sum = ctx.enter_context(tc.psum_pool(name="ps_sum", bufs=2))
        ctx.enter_context(tc.manual_schedule())

        rows = "(g p t) d -> g p t d"
        q_hbm = q[0, :, :].rearrange(rows, g=GROUPS, t=PACK)
        k_hbm = k[0, :, :].rearrange(rows, g=GROUPS, t=PACK)
        v_hbm = v[0, :, :].rearrange(rows, g=GROUPS, t=PACK)
        pos_hbm = pos.rearrange(rows, g=GROUPS, t=PACK)
        out_hbm = out_0[0, :, :].rearrange(rows, g=GROUPS, t=PACK)

        q_raw = [keep.tile([P, PACK, D], BF16, name="q_raw%d" % i, align_bytes=64) for i in range(GROUPS)]
        k_raw = [keep.tile([P, PACK, D], BF16, name="k_raw%d" % i, align_bytes=64) for i in range(GROUPS)]
        v_raw = [keep.tile([P, PACK, D], BF16, name="v_raw%d" % i, align_bytes=64) for i in range(GROUPS)]
        pos_sb = [per_tile.tile([P, S], BF16, name="pos_sb", align_bytes=64) for i in range(TILES)]
        g_sb = keep.tile([P, TILES], BF16, name="g_sb")

        def load(raw, hbm, grp, lo, hi):
            nc.sync.dma_start(out=raw[grp][:, lo:hi, :], in_=hbm[grp, :, lo:hi, :])

        def load_pos(n):
            nc.sync.dma_start(out=pos_sb[n][:], in_=pos_hbm[n // PACK, :, n % PACK, :])

        load(q_raw, q_hbm, 0, 0, 2)
        load(k_raw, k_hbm, 0, 0, 2)
        load(k_raw, k_hbm, 0, 2, 4)
        load(k_raw, k_hbm, 1, 0, 2)
        load(k_raw, k_hbm, 1, 2, 4)
        load_pos(0)
        load_pos(1)
        load(q_raw, q_hbm, 0, 2, 4)
        load_pos(2)
        load_pos(3)
        load(q_raw, q_hbm, 1, 0, 4)
        for n in range(4, TILES):
            load_pos(n)
        load(v_raw, v_hbm, 0, 0, 4)
        load(v_raw, v_hbm, 1, 0, 4)
        nc.sync.dma_start(
            out=g_sb[:].rearrange("p (g t) -> p g t", t=PACK),
            in_=g.rearrange("(g p t) -> p g t", g=GROUPS, t=PACK),
        )

        ident = keep.tile([P, P], F32, name="ident")
        make_identity(nc, ident[:])

        def mx_tiles(label, width):
            woven = keep.tile([P, width, PACK], BF16, name=label + "_woven", align_bytes=64)
            codes = keep.tile([P, width], U32, name=label + "_codes", align_bytes=64)
            scales = keep.tile([P, width], U8, name=label + "_scales", align_bytes=64)
            return woven, codes, scales

        def quantize(operand, lo, hi):
            woven, codes, scales = operand
            nc.vector.quantize_mx(
                out=codes[:, lo:hi].bitcast(FP8X4),
                scales=scales[:, lo:hi],
                in_=woven[:, lo:hi, :].rearrange("p c t -> p (c t)"),
            )

        k_mx = [mx_tiles("k%d" % i, K_PASS) for i in range(GROUPS)]
        q_mx = [mx_tiles("q%d" % i, 2 * P) for i in range(TILES // 2)]
        v_mx = [mx_tiles("v%d" % i, D) for i in range(GROUPS)]
        o_mx = [mx_tiles("o%d" % i, D) for i in range(GROUPS)]

        def turn_pair(raw, t, pool, label):
            bank = pool.tile([P, 2, 2 * P], F32, name=label)
            for s in range(2):
                words = raw[:, t + s, :].bitcast(F32)
                for u in range(2):
                    nc.tensor.transpose(bank[:, u, s * P : (s + 1) * P], words[:, u : D // 2 : 2], ident[:])
            return bank

        def weave_words(copy, bank, woven):
            copy(
                out=woven.rearrange("p c t -> p (c t)").bitcast(F32).rearrange("p (c u) -> p c u", u=2),
                in_=bank[:].rearrange("p u c -> p c u"),
            )

        def turn_q(pair, copy):
            bank = turn_pair(q_raw[pair // 2], 2 * (pair % 2), ps_turn, "turned")
            weave_words(copy, bank, q_mx[pair][0][:])

        def turn_k(grp, half, copy, pool, label):
            bank = turn_pair(k_raw[grp], 2 * half, pool, label)
            weave_words(copy, bank, k_mx[grp][0][:, half * 2 * P : (half + 1) * 2 * P, :])

        def weave_v(grp, half):
            cols = slice(half * D // 2, (half + 1) * D // 2)
            dst = v_mx[grp][0][:, cols, :]
            src = v_raw[grp][:, :, cols].rearrange("p t d -> p d t")
            if grp == 0:
                nc.gpsimd.tensor_scalar(out=dst, in0=src, scalar1=1.0, scalar2=0.0, op0=ALU.mult, op1=ALU.add)
            else:
                nc.scalar.copy(out=dst, in_=src)

        score_bank = {}
        neg_l = {}
        shift = {}
        weight = {}
        row_sum = {}
        row_inv = {}

        def scores(n, grps):
            cols = slice((n % 2) * P, (n % 2 + 1) * P)
            for grp in grps:
                bank = ps_main.tile([P, BANK], F32, name="main")
                nc.tensor.matmul_mx(
                    out=bank[:],
                    lhsT=q_mx[n // 2][1][:, cols].bitcast(FP8X4),
                    lhsT_scale=q_mx[n // 2][2][:, cols],
                    rhs=k_mx[grp][1][:].bitcast(FP8X4),
                    rhs_scale=k_mx[grp][2][:],
                    start=True,
                    stop=True,
                )
                score_bank[n, grp] = bank

        def add_pos(n, grp):
            if n not in neg_l:
                nl = ring.tile([P, S], F32, name="nl")
                neg_l[n] = nl
            half = slice(grp * BANK, (grp + 1) * BANK)
            nc.vector.scalar_tensor_tensor(
                out=neg_l[n][:, half].rearrange("p (t a) -> p t a", t=PACK),
                in0=score_bank[n, grp][:].rearrange("p (t a) -> p t a", t=PACK),
                scalar=-SCORE_SCALE,
                in1=pos_sb[n][:, half].rearrange("p (a t) -> p t a", t=PACK),
                op0=ALU.mult,
                op1=ALU.subtract,
            )

        def row_max(n):
            spare = ring.tile([P, S], F32, name="spare")
            sh = per_tile.tile([P, 1], F32, name="sh")
            nc.vector.tensor_scalar(
                out=spare[:], in0=neg_l[n][:], scalar1=SHIFT, scalar2=None, op0=ALU.add, op1=ALU.min, accum_out=sh[:]
            )
            shift[n] = sh

        def exponentials(n):
            et = per_tile.tile([P, S], F32, name="et")
            rt = per_tile.tile([P, 1], F32, name="rt")
            nc.scalar.activation(
                out=et[:], in_=neg_l[n][:], func=ACT.Exp, bias=shift[n][:], scale=-1.0, accum_out=rt[:]
            )
            weight[n] = et
            row_sum[n] = rt

        def row_reciprocal(n):
            ri = per_tile.tile([P, 1], F32, name="ri")
            nc.vector.reciprocal(out=ri[:], in_=row_sum[n][:])
            row_inv[n] = ri

        def row_normalise(n, engine, pieces):
            for i in range(pieces):
                cols = slice(i * S // pieces, (i + 1) * S // pieces)
                engine.tensor_scalar(
                    out=weight[n][:, cols],
                    in0=weight[n][:, cols],
                    scalar1=GROW,
                    scalar2=row_inv[n][:],
                    op0=ALU.mult,
                    op1=ALU.mult,
                )

        col_bank = [ps_sum.tile([P, PACK, P], F32, name="sum") for i in range(GROUPS)]

        def add_columns(n):
            for grp in range(GROUPS):
                for t in range(PACK):
                    c0 = (grp * PACK + t) * P
                    nc.tensor.matmul(
                        out=col_bank[grp][:, t, :],
                        lhsT=weight[n][:, c0 : c0 + P],
                        rhs=ident[:],
                        start=(n == 0 and t == 0),
                        stop=(n == TILES - 1 and t == PACK - 1),
                        is_transpose=True,
                    )

        turn_q(0, nc.vector.tensor_copy)
        turn_k(0, 0, nc.scalar.copy, ps_turn, "turned")
        quantize(q_mx[0], 0, 2 * P)
        turn_k(0, 1, nc.vector.tensor_copy, ps_main, "main")
        quantize(k_mx[0], 0, 2 * P)
        quantize(k_mx[0], 2 * P, K_PASS)
        turn_k(1, 0, nc.scalar.copy, ps_main, "main")
        turn_k(1, 1, nc.scalar.copy, ps_turn, "turned")
        scores(0, (0,))
        scores(1, (0,))
        turn_q(1, nc.scalar.copy)
        add_pos(0, 0)
        quantize(k_mx[1], 0, K_PASS)
        add_pos(1, 0)
        scores(0, (1,))
        scores(1, (1,))

        for n in range(TILES):
            if n < 2:
                turn_q(n + 2, nc.scalar.copy)
            add_pos(n, 1)
            if 0 < n < TILES - 1:
                add_pos(n + 1, 0)
            row_max(n)
            exponentials(n)
            if n < 3:
                quantize(q_mx[n + 1], 0, 2 * P)
            if n > 0:
                row_reciprocal(n - 1)
                row_normalise(n - 1, nc.vector if n == TILES - 1 else nc.gpsimd, 1)
            if n + 2 < TILES:
                scores(n + 2, (0, 1))
            if n >= 2:
                add_columns(n - 2)
            if n == 3 or n == 5:
                weave_v(0, n // 2 - 1)
        quantize(v_mx[0], 0, D)
        gain = keep.tile([P, TILES], F32, name="gain")
        nc.vector.tensor_scalar(out=gain[:], in0=g_sb[:], scalar1=GAIN_SCALE, scalar2=None, op0=ALU.mult)
        row_reciprocal(TILES - 1)
        row_normalise(TILES - 1, nc.vector, 2)
        add_columns(TILES - 2)
        add_columns(TILES - 1)
        weave_v(1, 0)
        weave_v(1, 1)

        col_sum = keep.tile([P, TILES], F32, name="col_sum")
        u = keep.tile([P, TILES], F32, name="u")
        u_row = keep.tile([P, S], F32, name="u_row")
        u_bank = []
        for grp in range(GROUPS):
            cols = slice(grp * PACK, (grp + 1) * PACK)
            nc.vector.tensor_reduce(out=col_sum[:, cols], in_=col_bank[grp][:], axis=AX.X, op=ALU.add)
            nc.vector.reciprocal(out=u[:, cols], in_=col_sum[:, cols])
            spread = ps_turn.tile([P, PACK, P], F32, name="turned")
            for t in range(PACK):
                b = grp * PACK + t
                nc.tensor.transpose(spread[:, t, :], u[:, b : b + 1].to_broadcast([P, P]), ident[:])
            u_bank.append(spread)

        mixed = {}
        mix_sum = {}
        mix_inv = {}
        deviation = {}
        turned = {}
        c_woven = {}
        c_codes = {}
        c_scales = {}

        def scale_columns(n):
            wt = ring.tile([P, S], F32, name="wt")
            st = per_tile.tile([P, 1], F32, name="st")
            nc.vector.scalar_tensor_tensor(
                out=wt[:],
                in0=weight[n][:],
                scalar=1.0,
                in1=u_row[:],
                op0=ALU.mult,
                op1=ALU.mult,
                accum_out=st[:],
            )
            mixed[n] = wt
            mix_sum[n] = st

        def scale_columns_first():
            wt = ring.tile([P, S], F32, name="wt")
            parts = per_tile.tile([P, GROUPS], F32, name="parts")
            for grp in range(GROUPS):
                half = slice(grp * BANK, (grp + 1) * BANK)
                spread = u_bank[grp][:].rearrange("p t a -> p (t a)")
                nc.vector.scalar_tensor_tensor(
                    out=wt[:, half],
                    in0=weight[0][:, half],
                    scalar=1.0,
                    in1=spread,
                    op0=ALU.mult,
                    op1=ALU.mult,
                    accum_out=parts[:, grp : grp + 1],
                )
                nc.scalar.copy(out=u_row[:, half], in_=spread)
            quantize(v_mx[1], 0, D)
            st = per_tile.tile([P, 1], F32, name="st")
            nc.vector.tensor_tensor(out=st[:], in0=parts[:, 0:1], in1=parts[:, 1:2], op=ALU.add)
            mixed[0] = wt
            mix_sum[0] = st

        def scale_rows(n):
            si = per_tile.tile([P, 1], F32, name="si")
            nc.vector.reciprocal(out=si[:], in_=mix_sum[n][:])
            dv = ring.tile([P, S], F32, name="dv")
            nc.scalar.activation(out=dv[:], in_=mixed[n][:], func=ACT.Copy, bias=-1.0 / S, scale=si[:])
            deviation[n] = dv

        def turn_mix(n):
            for grp in range(GROUPS):
                bank = ps_main.tile([P, PACK, P], F32, name="main")
                for t in range(PACK):
                    c0 = (grp * PACK + t) * P
                    nc.tensor.transpose(bank[:, t, :], deviation[n][:, c0 : c0 + P], ident[:])
                turned[n, grp] = bank

        def apply_gain(n):
            cw = ring.tile([P, GROUPS, P, PACK], BF16, name="cw", align_bytes=64)
            for grp in range(GROUPS):
                gain_cols = gain[:, grp * PACK : (grp + 1) * PACK]
                nc.vector.tensor_tensor(
                    out=cw[:, grp, :, :],
                    in0=turned[n, grp][:].rearrange("p t i -> p i t"),
                    in1=gain_cols.unsqueeze(1).to_broadcast([P, P, PACK]),
                    op=ALU.mult,
                )
            c_woven[n] = cw

        def quantize_c(n):
            cc = ring.tile([P, GROUPS * P], U32, name="cc", align_bytes=64)
            cs = ring.tile([P, GROUPS * P], U8, name="cs", align_bytes=64)
            nc.vector.quantize_mx(
                out=cc[:].bitcast(FP8X4), scales=cs[:], in_=c_woven[n][:].rearrange("p g i t -> p (g i t)")
            )
            c_codes[n] = cc
            c_scales[n] = cs

        def mix(n, bank, lo, hi):
            for grp in range(GROUPS):
                cols = slice(grp * P, (grp + 1) * P)
                nc.tensor.matmul_mx(
                    out=bank[:, 0 : hi - lo],
                    lhsT=c_codes[n][:, cols].bitcast(FP8X4),
                    lhsT_scale=c_scales[n][:, cols],
                    rhs=v_mx[grp][1][:, lo:hi].bitcast(FP8X4),
                    rhs_scale=v_mx[grp][2][:, lo:hi],
                    start=(grp == 0),
                    stop=(grp == GROUPS - 1),
                )

        out_sb = [keep.tile([P, PACK, D], F32, name="out_sb%d" % i) for i in range(GROUPS)]

        def store_rows(n):
            grp, t = n // PACK, n % PACK
            nc.sync.dma_start(out=out_hbm[grp, :, t, :], in_=out_sb[grp][:, t, :])

        def weave_out(grp, lo, hi, copy):
            copy(out=o_mx[grp][0][:, lo:hi, :], in_=out_sb[grp][:, :, lo:hi].rearrange("p t d -> p d t"))

        def store_planes(grp):
            codes, scales = o_mx[grp][1], o_mx[grp][2]
            nc.sync.dma_start(
                out=out_1[grp, :, :, :].rearrange("p m t -> p (m t)").bitcast(I32), in_=codes[:].bitcast(I32)
            )
            for quad in range(4):
                nc.sync.dma_start(
                    out=out_2[grp, 4 * quad : 4 * quad + 4, :].bitcast(I32),
                    in_=scales[32 * quad : 32 * quad + 4, :].bitcast(I32),
                )

        LEAD = 3
        for n in range(LEAD):
            if n == 0:
                scale_columns_first()
            else:
                scale_columns(n)
            scale_rows(n)
            if n < 2:
                turn_mix(n)
        for n in range(TILES):
            if n <= TILES - LEAD:
                apply_gain(n)
            if n == 0:
                turn_mix(2)
            if n + LEAD < TILES:
                scale_columns(n + LEAD)
            elif n + 1 < TILES:
                apply_gain(n + 1)
            quantize_c(n)
            if n + LEAD < TILES:
                scale_rows(n + LEAD)
            if 0 < n < TILES - 2:
                turn_mix(n + 2)
            if n < TILES - 1:
                bank = ps_sum.tile([P, BANK], F32, name="sum")
                mix(n, bank, 0, D)
                nc.scalar.copy(out=out_sb[n // PACK][:, n % PACK, :], in_=bank[:])
                store_rows(n)
            if n == 3 or n == 4:
                weave_out(0, (n - 3) * D // 2, (n - 2) * D // 2, nc.scalar.copy)

        last = TILES - 1
        half = D // 2
        low = ps_sum.tile([P, BANK], F32, name="sum")
        high = ps_turn.tile([P, BANK], F32, name="turned")
        mix(last, low, 0, half)
        mix(last, high, half, D)
        quantize(o_mx[0], 0, D)
        store_planes(0)
        nc.vector.tensor_copy(out=out_sb[1][:, PACK - 1, 0:half], in_=low[:, 0:half])
        nc.scalar.copy(out=out_sb[1][:, PACK - 1, half:D], in_=high[:, 0:half])
        store_rows(last)
        weave_out(1, 0, half, nc.vector.tensor_copy)
        weave_out(1, half, D, nc.scalar.copy)
        quantize(o_mx[1], 0, half)
        quantize(o_mx[1], half, D)
        store_planes(1)
